import numpy as np
import ml_dtypes


def mxq(x, axis, fmt="e4m3"):
    dtype, down = {"e4m3": (ml_dtypes.float8_e4m3fn, 7), "e5m2": (ml_dtypes.float8_e5m2, 14)}[fmt]
    v = np.moveaxis(np.asarray(x, np.float32).astype(ml_dtypes.bfloat16).astype(np.float64), axis, -1)
    blocks = v.reshape(v.shape[:-1] + (-1, 32))
    amax = np.abs(blocks).max(-1, keepdims=True)
    byte = np.maximum(np.where(amax > 0, np.frexp(amax)[1] - 1 + 127, 0) - down, 1)
    scale = np.exp2(byte - 127.0)
    codes = (blocks / scale).astype(np.float32).astype(dtype).astype(np.float64)
    return np.moveaxis((codes * scale).reshape(v.shape), -1, axis)


WIDE = False


def mx_kscale(k):
    if not WIDE:
        return np.ones(k)
    levels = np.array([30, -30])
    if k % 512:
        return np.exp2(np.random.permutation(np.resize(levels, k // 32))).repeat(32)
    a = np.empty((k // 512, 16))
    for p in range(k // 512):
        a[p, :8] = np.random.permutation(np.resize(levels, 8))
        for g in range(8):
            far = levels[np.abs(levels - a[p, g]) >= 10]
            a[p, g + 8] = far[np.random.randint(len(far))]
    return np.exp2(a.ravel()).repeat(32)


def f64(x):
    return np.asarray(x).astype(np.float64)


def striped(idx):
    return np.tile(np.asarray(idx).reshape(-1, 16).T, (8, 1)).astype(np.uint16)


def unstriped(offs):
    return offs[:16].T.reshape(-1).astype(np.int64)


def striped8(idx):
    return np.asarray(idx).reshape(8, -1, 16).transpose(0, 2, 1).reshape(128, -1).astype(np.uint16)


def unstriped8(offs):
    return offs.reshape(8, 16, -1).transpose(0, 2, 1).reshape(8, -1).astype(np.int64)


def pick8(x, idx, run):
    r = np.arange(len(x))
    return x[r[:, None], idx[r % (8 * run) // run]]


E2M1 = np.array([0.0, 0.5, 1.0, 1.5, 2.0, 3.0, 4.0, 6.0, -0.0, -0.5, -1.0, -1.5, -2.0, -3.0, -4.0, -6.0])


def pack_weight(w, fmt):
    k, n = w.shape
    w = f64(np.asarray(w, np.float32).astype(ml_dtypes.bfloat16)).reshape(k // 32, 32, n)
    amax = np.abs(w).max(1)
    if fmt in ("e4m3", "e5m2"):
        byte = np.frexp(amax)[1] - 1 + 127 - (7 if fmt == "e4m3" else 14)
    else:
        mant, ex = np.frexp(amax / 6.0)
        byte = np.where(mant > 0.5, ex, ex - 1) + 127
    byte = np.clip(np.where(amax > 0, byte, 1), 1, 254)
    scaled = (w * np.exp2(127.0 - byte)[:, None, :]).reshape(k, n).astype(np.float32)
    by_word = np.ascontiguousarray(scaled.reshape(k // 512, 128, 4, n).transpose(0, 1, 3, 2))
    if fmt in ("e4m3", "e5m2"):
        words = by_word.astype(ml_dtypes.float8_e4m3fn if fmt == "e4m3" else ml_dtypes.float8_e5m2).view(np.uint8)
    else:
        c = by_word.astype(ml_dtypes.float4_e2m1fn).view(np.uint8) & 0xF
        words = (c[..., 0::2] | (c[..., 1::2] << 4)).reshape(k // 512, 128, 2 * n)
    return np.ascontiguousarray(words), np.ascontiguousarray(byte.astype(np.uint8).reshape(k // 512, 16, n))


def unpack_weight(words, scales, fmt):
    g, _, n = scales.shape
    words = np.ascontiguousarray(words).reshape(g, 128, n, -1)
    if fmt in ("e4m3", "e5m2"):
        vals = words.view(ml_dtypes.float8_e4m3fn if fmt == "e4m3" else ml_dtypes.float8_e5m2).astype(np.float64)
    else:
        nib = np.empty((g, 128, n, 4), np.uint8)
        nib[..., 0::2] = words & 0xF
        nib[..., 1::2] = words >> 4
        vals = E2M1[nib]
    vals = vals * np.repeat(np.exp2(scales.astype(np.float64) - 127.0), 8, axis=1)[..., None]
    return vals.transpose(0, 1, 3, 2).reshape(g * 512, n)


K, T, J, R, F, Z, C, O, D, N = 512, 1024, 256, 512, 512, 1024, 512, 256, 512, 256


def setup_inputs():
    n = np.random.standard_normal
    idx = np.random.permutation(T)[:J]
    idx2 = np.random.permutation(Z)[:J]
    idx3 = np.stack([np.random.permutation(C)[:J] for _ in range(8)])
    idx4 = np.stack([np.random.permutation(C)[:O] for _ in range(8)])
    fk = mx_kscale(K)
    ff = mx_kscale(F)
    fr = mx_kscale(R)
    xtp = pack_weight(n((K, T)) / fk[:, None], "e5m2")
    xop = pack_weight(n((F, Z)) / ff[:, None], "e4m3")
    wp = pack_weight(n((K, R)) * 1 / np.sqrt(K) * fk[:, None] * fr, "e2m1")
    w2p = pack_weight(n((K, R)) * 1 / np.sqrt(K) * fk[:, None] * fr, "e4m3")
    w0p = pack_weight(n((F, R)) * 1 / np.sqrt(F) * ff[:, None] * fr, "e4m3")
    wbp = pack_weight(n((R, N)) * 1 / np.sqrt(R) / fr[:, None], "e2m1")
    return {
        "xt_words": xtp[0],
        "xt_scales": xtp[1],
        "xo_words": xop[0],
        "xo_scales": xop[1],
        "w_words": wp[0],
        "w_scales": wp[1],
        "w2_words": w2p[0],
        "w2_scales": w2p[1],
        "w0_words": w0p[0],
        "w0_scales": w0p[1],
        "wb_words": wbp[0],
        "wb_scales": wbp[1],
        "offs": striped(idx),
        "offs2": striped(idx2),
        "offs3": striped8(idx3),
        "offs4": striped8(idx4),
    }


def reference(xt_words, xt_scales, xo_words, xo_scales, w_words, w_scales, w2_words, w2_scales, w0_words, w0_scales, wb_words, wb_scales, offs, offs2, offs3, offs4):
    idx = unstriped(offs)
    idx2 = unstriped(offs2)
    idx3 = unstriped8(offs3)
    idx4 = unstriped8(offs4)
    xtu = unpack_weight(xt_words, xt_scales, "e5m2")
    xou = unpack_weight(xo_words, xo_scales, "e4m3")
    wu = unpack_weight(w_words, w_scales, "e2m1")
    w2u = unpack_weight(w2_words, w2_scales, "e4m3")
    w0u = unpack_weight(w0_words, w0_scales, "e4m3")
    wbu = unpack_weight(wb_words, wb_scales, "e2m1")
    xtidxg = xtu[:, idx]
    a = wu.T @ xtidxg
    xoidx2g = xou[:, idx2]
    b = w2u.T @ xtidxg + w0u.T @ xoidx2g
    pa = np.zeros((R, C))
    pa[np.arange(R)[:, None], idx3[np.arange(R) % 512 // 64]] = a
    h1 = pick8(pa, idx4, 64)
    hid = np.concatenate([b, h1], axis=1)
    hidq = mxq(hid, 0, "e4m3")
    p = wbu.T @ hidq
    return p

from contextlib import ExitStack

import concourse.mybir as mybir
from concourse.masks import make_identity

K, T, J, R, Z, C, O, D, N = 512, 1024, 256, 512, 1024, 512, 256, 512, 256
FLOPS = 2 * (3 * K * R * J + R * N * D)

F32 = mybir.dt.float32
BF16 = mybir.dt.bfloat16
I32 = mybir.dt.int32
U32 = mybir.dt.uint32
U16 = mybir.dt.uint16
U8 = mybir.dt.uint8
E4M3 = mybir.dt.float8_e4m3fn_x4
E5M2 = mybir.dt.float8_e5m2_x4
E2M1 = mybir.dt.float4_e2m1fn_x4
COPY = mybir.ActivationFunctionType.Copy

P = 128
PACK = 4
HALF = 128
HCOL = HALF // 16


def tile_list_joinedreads_kernel(tc, xt_words, xt_scales, xo_words, xo_scales, w_words, w_scales, w2_words, w2_scales, w0_words, w0_scales, wb_words, wb_scales, offs, offs2, offs3, offs4, out):
    nc = tc.nc
    with ExitStack() as ctx:
        keep = ctx.enter_context(tc.tile_pool(name="keep", bufs=1))
        reuse = ctx.enter_context(tc.tile_pool(name="reuse", bufs=1))
        psum = ctx.enter_context(tc.psum_pool(name="psum", bufs=1))

        def sb(name, shape, dtype):
            return keep.tile(shape, dtype, name=name, align_bytes=64)

        def bank(name, tag, shape):
            return psum.tile(shape, F32, name=name, tag=tag)

        def load_list(name, src):
            t = keep.tile([P, 16], U16, name=name)
            nc.sync.dma_start(t[:], src)
            return t

        def load_words(t, src):
            flat = src[0].rearrange("p n t -> p (n t)") if src.ndim == 4 else src[0]
            nc.sync.dma_start(t[:], flat.bitcast(I32))
            return t

        def load_plane(t, src):
            for q in range(4):
                nc.sync.dma_start(t[32 * q : 32 * q + 4, :], src[0, 4 * q : 4 * q + 4, :].bitcast(I32))
            return t[:].bitcast(U8)

        out_v = out.rearrange("(g p) d -> p g d", p=P)

        l1 = load_list("l1", offs)
        xs_win = sb("xs_win", [P, T // 4], I32)
        for q in range(4):
            rows = xt_scales[0, 4 * q : 4 * q + 4, :].bitcast(I32)
            nc.scalar.dma_start(xs_win[32 * q : 32 * q + 32, :], rows.unsqueeze(0).to_broadcast([8, 4, T // 4]))
        ws_stage = sb("ws_stage", [4, 4, R // 4], I32)
        nc.sync.dma_start(ws_stage[:], w_scales[0].bitcast(I32).rearrange("(q r) c -> r q c", r=4))
        xt_win = load_words(sb("xt_win", [P, T], I32), xt_words)
        w_raw = load_words(reuse.tile([P, R // 2], I32, name="w_raw", align_bytes=64, offset=1536), w_words)
        l3 = load_list("l3", offs3)

        ws_plane = sb("ws_plane", [P, R // 4], I32)
        xos_win = sb("xos_win", [P, Z // 4], I32)
        w2s_plane = sb("w2s_plane", [P, R // 4], I32)
        w0s_plane = sb("w0s_plane", [P, R // 4], I32)
        wbs_plane = sb("wbs_plane", [P, N // 4], I32)
        boards = [sb("board%d" % t, [P, C], F32) for t in range(2)]
        for t in (xos_win, w2s_plane, w0s_plane, wbs_plane):
            nc.gpsimd.memset(t[:], 0)
        nc.vector.memset(ws_plane[:], 0)
        for t in range(2):
            nc.vector.memset(boards[t][:], 0.0)
        ident = sb("ident", [P, P], F32)
        make_identity(nc, ident[:])

        xo_win = load_words(reuse.tile([P, Z], I32, name="xo_win", align_bytes=64, offset=4096), xo_words)
        l2 = load_list("l2", offs2)
        xos_view = load_plane(xos_win, xo_scales)
        w2w = load_words(sb("w2w", [P, R], I32), w2_words)
        w2s = load_plane(w2s_plane, w2_scales)
        w0w = load_words(sb("w0w", [P, R], I32), w0_words)
        l4 = load_list("l4", offs4)
        w0s = load_plane(w0s_plane, w0_scales)
        wbw = load_words(sb("wbw", [P, N // 2], I32), wb_words)
        wbs = load_plane(wbs_plane, wb_scales)

        for q in range(4):
            nc.vector.tensor_copy(ws_plane[32 * q : 32 * q + 4, :], ws_stage[:, q, :])
        xts = sb("xts", [P, J], U8)
        nc.vector.tensor_copy(xts[:], xs_win[:].bitcast(U8).indirect(l1[:]))
        ws_by_t = ws_plane[:].bitcast(U8).rearrange("p (m t) -> p t m", t=PACK)
        w_by_t = w_raw[:].bitcast(U16).rearrange("p (m t) -> p t m", t=PACK)
        ws_dealt = [keep.tile([P, P], U8, name="ws_dealt%d" % t, tag="ws_dealt%d" % t, align_bytes=64) for t in range(PACK)]
        w_first = sb("w_first", [P, P], U16)
        w_rest = keep.tile([P, PACK - 1, P], U16, name="w_rest", tag="w_rest", align_bytes=64)
        for t in range(PACK):
            nc.gpsimd.tensor_copy(ws_dealt[t][:], ws_by_t[:, t, :])

        xtw = sb("xtw", [P, J], U32)
        xt_view = xt_win[:].bitcast(U32)
        nc.vector.tensor_copy(xtw[:, :HALF], xt_view.indirect(l1[:, :HCOL]))
        nc.scalar.copy(w_first[:], w_by_t[:, 0, :])
        nc.vector.tensor_copy(xtw[:, HALF:], xt_view.indirect(l1[:, HCOL:]))
        nc.scalar.copy(w_rest[:], w_by_t[:, 1:, :])
        for t in range(2, PACK):
            boards.append(reuse.tile([P, C], F32, name="board%d" % t, align_bytes=64, offset=2048 * (t - 2)))
            nc.gpsimd.memset(boards[t][:], 0.0)

        def first_stage(dst, t, cols):
            wt = w_first[:] if t == 0 else w_rest[:, t - 1, :]
            st = ws_dealt[t][:]
            nc.tensor.matmul_mx(out=dst, lhsT=wt.bitcast(E2M1), lhsT_scale=st, rhs=xtw[:, cols].bitcast(E5M2), rhs_scale=xts[:, cols], start=True, stop=True)

        lo, hi, whole = slice(0, HALF), slice(HALF, J), slice(0, J)
        a0_lo_ps = bank("a0_lo_ps", "b0", [P, HALF])
        first_stage(a0_lo_ps[:], 0, lo)
        a0_hi_ps = bank("a0_hi_ps", "b2", [P, HALF])
        first_stage(a0_hi_ps[:], 0, hi)
        a1_ps = bank("a1_ps", "b1", [P, J])
        first_stage(a1_ps[:], 1, whole)
        a2_ps = bank("a2_ps", "b3", [P, J])
        first_stage(a2_ps[:], 2, whole)
        a3_ps = bank("a3_ps", "b4", [P, J])
        first_stage(a3_ps[:], 3, whole)

        a0_lo = sb("a0_lo", [P, HALF], F32)
        a1 = sb("a1", [P, J], F32)
        a0_hi = sb("a0_hi", [P, HALF], F32)
        a2 = sb("a2", [P, J], F32)
        a3 = sb("a3", [P, J], F32)
        nc.vector.tensor_copy(a0_lo[:], a0_lo_ps[:])
        nc.vector.tensor_copy(a0_hi[:], a0_hi_ps[:])
        nc.vector.tensor_copy(a1[:], a1_ps[:])
        nc.vector.tensor_copy(a2[:], a2_ps[:])
        nc.vector.tensor_copy(a3[:], a3_ps[:])

        nc.scalar.activation(boards[0][:].indirect(l3[:, :HCOL]), a0_lo[:], COPY)
        nc.scalar.activation(boards[0][:].indirect(l3[:, HCOL:]), a0_hi[:], COPY)
        nc.scalar.activation(boards[1][:].indirect(l3[:]), a1[:], COPY)
        nc.scalar.activation(boards[2][:].indirect(l3[:]), a2[:], COPY)
        nc.scalar.activation(boards[3][:].indirect(l3[:]), a3[:], COPY)

        xos = keep.tile([P, J], U8, name="xos", tag="ws_dealt1", align_bytes=64)
        xow = keep.tile([P, J], U32, name="xow", tag="ws_dealt2", align_bytes=64)
        nc.vector.tensor_copy(xos[:], xos_view.indirect(l2[:]))
        nc.vector.tensor_copy(xow[:], xo_win[:].bitcast(U32).indirect(l2[:]))
        bt_ps = [bank("bt_ps%d" % h, "b%d" % (3 + h), [P, R]) for h in range(2)]
        for h, cols in enumerate((lo, hi)):
            nc.tensor.matmul_mx(out=bt_ps[h][:], lhsT=xtw[:, cols].bitcast(E5M2), lhsT_scale=xts[:, cols], rhs=w2w[:].bitcast(E4M3), rhs_scale=w2s, start=True, stop=False)
        for h, cols in enumerate((lo, hi)):
            nc.tensor.matmul_mx(out=bt_ps[h][:], lhsT=xow[:, cols].bitcast(E4M3), lhsT_scale=xos[:, cols], rhs=w0w[:].bitcast(E4M3), rhs_scale=w0s, start=False, stop=True)

        early = reuse.tile([P, O + R], BF16, name="early", align_bytes=64, offset=4096)
        nc.vector.tensor_copy(early[:, :O], boards[0][:].indirect(l4[:]))
        bt1 = keep.tile([P, R], BF16, name="bt1", tag="late", align_bytes=64)
        bt = [early[:, O:], bt1[:]]
        turn_ps = bank("turn_ps", "b6", [P, 2, 2, HALF])
        for h in range(2):
            nc.vector.tensor_copy(bt[h].rearrange("j (u m e) -> j u m e", u=2, e=2), bt_ps[h][:].rearrange("j (m u e) -> j u m e", u=2, e=2))
            pairs = bt[h].bitcast(F32)
            for u in range(2):
                nc.tensor.transpose(turn_ps[:, h, u, :], pairs[:, u * P : (u + 1) * P], ident[:])
        nc.vector.tensor_copy(early[:, O : 2 * O], boards[1][:].indirect(l4[:]))
        hid_b = sb("hid_b", [P, J * PACK], BF16)
        nc.vector.tensor_copy(hid_b[:].bitcast(F32).rearrange("m (h j u) -> m h j u", h=2, u=2), turn_ps[:].rearrange("m h u j -> m h j u"))
        late = keep.tile([P, 2, O], BF16, name="late", tag="late", align_bytes=64)
        nc.vector.tensor_copy(late[:, 0, :], boards[2][:].indirect(l4[:]))
        hid_r = sb("hid_r", [P, O, PACK], BF16)
        nc.vector.tensor_copy(hid_r[:, :, 0:2], early[:, : 2 * O].rearrange("p (t o) -> p o t", t=2))

        def quantize(name, hid):
            width = hid.shape[1] // PACK
            codes = sb(name + "_codes", [P, width], U32)
            scales = sb(name + "_scales", [P, width], U8)
            nc.vector.quantize_mx(out=codes[:].bitcast(E4M3), scales=scales[:], in_=hid)
            return codes, scales

        def second_stage(name, tag, codes, scales):
            acc = bank(name, tag, [P, 2, codes.shape[1]])
            for g in range(2):
                nc.tensor.matmul_mx(out=acc[:, g, :], lhsT=wbw[:].bitcast(U16)[:, g * P : (g + 1) * P].bitcast(E2M1), lhsT_scale=wbs[:, g * P : (g + 1) * P], rhs=codes[:].bitcast(E4M3), rhs_scale=scales[:], start=True, stop=True)
            return acc

        ob_ps = second_stage("ob_ps", "b7", *quantize("qb", hid_b[:]))
        ob = sb("ob", [P, 2, J], F32)

        nc.vector.tensor_copy(late[:, 1, :HALF], boards[3][:].indirect(l4[:, :HCOL]))
        nc.scalar.activation(late[:, 1, HALF:], boards[3][:].indirect(l4[:, HCOL:]), COPY)
        nc.scalar.copy(ob[:], ob_ps[:])
        nc.sync.dma_start(out_v[:, :, :J], ob[:])
        for cols in (lo, hi):
            nc.vector.tensor_copy(hid_r[:, cols, 2:4], late[:, :, cols].rearrange("p t o -> p o t"))
        quant = [quantize("qr%d" % h, hid_r[:, cols, :].rearrange("p o t -> p (o t)")) for h, cols in enumerate((lo, hi))]
        for h in range(2):
            acc = second_stage("or_ps%d" % h, "b%d" % h, *quant[h])
            res = sb("or%d" % h, [P, 2, HALF], F32)
            if h == 0:
                nc.vector.tensor_copy(res[:], acc[:])
                nc.sync.dma_start(out_v[:, :, J : J + HALF], res[:])
            else:
                nc.scalar.copy(res[:], acc[:])
                nc.scalar.dma_start(out_v[:, :, J + HALF :], res[:])
